import numpy as np, ml_dtypes
CORES = [10,34,74,98]
N = 4
import mx_ref
BF = ml_dtypes.bfloat16
def entries(a):
    return np.ascontiguousarray(a.T).reshape(-1)
def table(e):
    return np.ascontiguousarray(np.reshape(e, (-1, 16)).T).astype(np.int32)
def gentries(a):
    return np.ascontiguousarray(a.reshape(8, 16, -1).transpose(0, 2, 1)).reshape(8, -1)
def gtable(e):
    e = np.asarray(e); return np.ascontiguousarray(e.reshape(8, -1, 16).transpose(0, 2, 1)).reshape(128, -1).astype(np.int32)
def tile(rs):
    return np.stack(rs, axis=2).reshape(128, -1).astype(BF)
def cut(t, i, w=512):
    return t[:, w * i:w * i + w]
def f(rng, *shape):
    return mx_ref.flush((rng.standard_normal(shape, dtype=np.float32) * np.exp2(rng.integers(-2, 3, shape[:-1] + (1,)))).astype(BF))
def wide(rng, *shape, cols=0):
    v = rng.standard_normal(shape, dtype=np.float32) * np.exp2(rng.integers(-12, 13, shape)).astype(np.float32)
    if cols: v *= np.repeat(np.exp2(rng.integers(-cols, cols + 1, shape[:-2] + (1, shape[-1] // 4))) * (rng.random(shape[:-2] + (1, shape[-1] // 4)) > 0.0625), 4, axis=-1).astype(np.float32)
    return mx_ref.flush(v.astype(BF))
T, CAPP, P = 512, 96, 256
SL = N * CAPP
G = 8
def pieces(rng, how):
    if how == "ones": n = np.ones((G, SL), int)
    elif how == "full":
        n = T - rng.integers(0, 8, (G, SL)); n[:, ::4] = T
    elif how == "powers":
        k = [1 << i for i in range(T.bit_length())]; k = sorted(set(k + [i + 1 for i in k if i < T]))
        n = rng.permuted(np.tile(np.resize(k, SL), (G, 1)), axis=1)
    else: n = np.where(rng.random((G, SL)) < 0.5, rng.integers(1, T + 1, (G, SL)), np.clip(np.exp2(rng.uniform(0, T.bit_length() - 1, (G, SL))).astype(int), 1, T))
    s = rng.integers(0, T - n + 1)
    if how == "full": s[:] = 0
    if how == "nested":
        for g in range(G):
            for r in range(N):
                m = rng.integers(0, T)
                b = np.sort(rng.choice(rng.integers(0, m + 1, 16), CAPP)); e = np.sort(rng.choice(rng.integers(m, T, 16), CAPP))[::-1]
                k = r * CAPP + rng.permutation(CAPP); s[g, k] = b; n[g, k] = e - b + 1
    return s, n
def lists(rng, how="any", every=False):
    held = np.zeros((N, N, CAPP), bool)
    for r in range(N):
        n = rng.integers(0, CAPP + 1, N); n[(r + rng.integers(1, N)) % N] = CAPP
        for q in range(N): held[q, r, rng.permutation(CAPP)[:CAPP if every else n[q]]] = True
    d = {"lo": [], "ln": [], "pf": [], "pg": []}
    for q in range(N):
        s, n = pieces(rng, how); e = ~held[q].reshape(-1)
        s[:, e] = -1; n[:, e] = 0
        d["lo"].append(gtable(s)); d["ln"].append(gtable(n))
    who = rng.permutation(N)
    for r in range(N):
        k = rng.permutation(np.flatnonzero(held[:, r]))
        first = rng.permutation(np.resize(k, P))
        second = np.where(rng.random(P) < 0.25, -1, rng.choice(k, P))
        if how == "ones":
            if r == who[0]:
                first[rng.permutation(P)[:P // 2]] = k[0]; second[rng.permutation(P)[:P // 2]] = k[0]
            if r == who[1]: second[:] = -1
            if r == who[2]: second = rng.choice(k, P)
        d["pf"].append(table(first))
        d["pg"].append(table(second))
    return {k: np.stack(t) for k, t in d.items()}
def setup_inputs(rng):
    return {"x": f(rng, N, 128, 4 * T), "a": f(rng, N, 128, 2048), "u": f(rng, N, 128, 512), "v": f(rng, N, 128, 512), **lists(rng)}
def setup_inputs_ones(rng):
    return {**setup_inputs(rng), **lists(rng, "ones")}
def setup_inputs_full(rng):
    return {**setup_inputs(rng), **lists(rng, "full", True)}
def setup_inputs_powers(rng):
    return {**setup_inputs(rng), **lists(rng, "powers", True)}
def setup_inputs_nested(rng):
    return {**setup_inputs(rng), **lists(rng, "nested", True)}
def setup_inputs_spread(rng):
    d = setup_inputs(rng); d["x"] = wide(rng, N, 128, 4 * T, cols=8); return d
def check_inputs(d):
    b = []; held = []
    for q in range(N):
        s, n = gentries(d["lo"][q]).reshape(G, -1), gentries(d["ln"][q]).reshape(G, -1)
        e = s == -1; held.append(~e[0])
        if s.min() < -1 or s.max() >= T or (e != e[:1]).any(): b.append("lo")
        if (n[e] != 0).any() or (n[~e] < 1).any() or (n[~e] > T - s[~e]).any(): b.append("ln")
    for r in range(N):
        h = np.concatenate([held[q][r * CAPP:r * CAPP + CAPP] for q in range(N)])
        for k, least in (("pf", 0), ("pg", -1)):
            j = entries(d[k][r])
            if j.min() < least or j.max() >= SL or not h[j[(j >= 0) & (j < SL)]].all(): b.append(k)
    return b
def reference(x, a, u, v, lo, ln, pf, pg):
    sent = []
    for q in range(N):
        X = mx_ref.quantize(x[q])
        Z = np.stack([mx_ref.matmul(mx_ref.quantize(np.ascontiguousarray(cut(a[q], i))), X) for i in range(4)])
        h = np.maximum(Z, np.float32(0)) * np.float32(0.05)
        s, n = gentries(lo[q]), gentries(ln[q])
        R = np.zeros((4, 128, SL), np.float32)
        for k in range(SL):
            for g in range(8):
                if n[g, k]: R[:, 16 * g:16 * g + 16, k] = h[:, 16 * g:16 * g + 16, s[g, k]:s[g, k] + n[g, k]].max(axis=2)
        sent.append([mx_ref.quantize(np.ascontiguousarray(tile([R[i][:, CAPP * r:CAPP * r + CAPP] for i in range(4)]))) for r in range(N)])
    y = np.zeros((N, 128, P), np.float32)
    for r in range(N):
        V, U = mx_ref.quantize(v[r]), mx_ref.quantize(u[r])
        zv = np.concatenate([mx_ref.matmul(V, sent[q][r]) for q in range(N)], axis=1)
        zu = np.concatenate([mx_ref.matmul(U, sent[q][r]) for q in range(N)], axis=1)
        first, second = entries(pf[r]), entries(pg[r])
        y[r] = zv[:, first]
        two = second >= 0
        y[r][:, two] += zu[:, second[two]]
    return {"y": y}

@@ -1,0 +1,346 @@
+from concourse.bass import DstId, RemoteDMATransfer, IndirectOffsetOnAxis
+from concourse.mybir import dt, AluOpType, ActivationFunctionType
+
+A = AluOpType
+F = ActivationFunctionType
+N = 4
+CAPP = 96
+P = 256
+SL = N * CAPP
+X = 512
+LV = (2, 4, 6)
+PT = {2: 3, 4: 2, 6: 1}
+ST = {2: 5, 4: 6, 6: 7}
+MT = 8
+H0, PB, SB, NT = 4, 0, 8, 12
+W = NT * X
+
+SCRATCH = {
+    "xs": ("sbuf", [128, 2048], "bfloat16"),
+    "ab": ("sbuf", [128, 2048], "bfloat16"),
+    "uv": ("sbuf", [128, 1024], "bfloat16"),
+    "xq": ("sbuf", [128, 512], "float8_e4m3fn_x4"),
+    "xc": ("sbuf", [128, 512], "uint8"),
+    "aq": ("sbuf", [128, 512], "float8_e4m3fn_x4"),
+    "ac": ("sbuf", [128, 512], "uint8"),
+    "uvq": ("sbuf", [128, 256], "float8_e4m3fn_x4"),
+    "uvc": ("sbuf", [128, 256], "uint8"),
+    "ps": ("psum", [128, 4096], "float32"),
+    "tb": ("sbuf", [128, 4 * W], "bfloat16"),
+    "mk": ("sbuf", [128, 3 * X], "bfloat16"),
+    "mi": ("sbuf", [128, 2 * SL], "bfloat16"),
+    "lnb": ("sbuf", [128, 24], "int32"),
+    "lob": ("sbuf", [128, 24], "int32"),
+    "wt": ("sbuf", [128, 2, 2, 5, 24], "int32"),
+    "vt": ("sbuf", [128, 2, 3, 24], "float32"),
+    "dd": ("sbuf", [128, 4, 24], "float32"),
+    "cc": ("sbuf", [128, 2, 24], "float32"),
+    "eq": ("sbuf", [128, 3, 24], "float32"),
+    "qq": ("sbuf", [128, 3, 24], "float32"),
+    "mb": ("sbuf", [128, 3, 24], "float32"),
+    "mx": ("sbuf", [128, 3, 24], "float32"),
+    "offl": ("sbuf", [128, 24], "uint16"),
+    "offr": ("sbuf", [128, 24], "uint16"),
+    "offm": ("sbuf", [128, 24], "uint16"),
+    "ga": ("sbuf", [128, 8 * SL], "bfloat16"),
+    "gb": ("sbuf", [128, 8 * SL], "bfloat16"),
+    "t": ("sbuf", [128, 4 * SL], "bfloat16"),
+    "tq": ("sbuf", [128, 192], "float8_e4m3fn_x4"),
+    "tc": ("sbuf", [128, 192], "uint8"),
+    "tq1": ("sbuf", [128, 128], "float8_e4m3fn_x4"),
+    "tc1": ("sbuf", [128, 128], "uint8"),
+    "tq2": ("sbuf", [128, 128], "float8_e4m3fn_x4"),
+    "tc2": ("sbuf", [128, 128], "uint8"),
+    "rq": ("sbuf", [128, 288], "float8_e4m3fn_x4"),
+    "rc": ("sbuf", [128, 288], "uint8"),
+    "pidx": ("sbuf", [128, 1], "int32"),
+    "pid16": ("sbuf", [128, 1], "int32"),
+    "pp": ("sbuf", [128, 32], "int32"),
+    "pw": ("sbuf", [128, 32], "float32"),
+    "pn": ("sbuf", [128, 16], "float32"),
+    "offf": ("sbuf", [128, 16], "uint16"),
+    "offg": ("sbuf", [128, 16], "uint16"),
+    "zvs": ("sbuf", [128, SL], "float32"),
+    "zus": ("sbuf", [128, SL + 8], "float32"),
+    "y1": ("sbuf", [128, P], "float32"),
+    "ys": ("sbuf", [128, P], "float32"),
+}
+SEMAPHORES = ["sv", "st", "sa", "sg", "dlo", "dln", "dx0", "dx1", "da0", "da1", "da2", "du", "dv", "dy",
+              "gi", "arre", "arrl", "loc"]
+
+
+def rank_program(g, core, T, topo):
+    q = T.rank_of(core)
+    if q is None:
+        return
+    v, ten, act, sy, s = g.vector, g.tensor, g.scalar, g.sync, T.sem
+    cnt = {"sv": 0, "st": 0, "sa": 0, "sg": 0}
+    seen = {}
+
+    def done(ins, name):
+        cnt[name] += 1
+        ins.then_inc(s[name], 1)
+        return (name, cnt[name])
+
+    def need(eng, en, *evs):
+        for name, val in evs:
+            if seen.get((en, name), 0) < val:
+                eng.wait_ge(s[name], val)
+                seen[(en, name)] = val
+
+    def V(ins):
+        return done(ins, "sv")
+
+    def vw(*evs):
+        need(v, "v", *evs)
+
+    sy.dma_start(T.lob[:], T.lo[:]).then_inc(s.dlo, 16)
+    act.dma_start(T.lnb[:], T.ln[:]).then_inc(s.dln, 16)
+    sy.dma_start(T.xs[:, 0:1024], T.x[:, 0:1024]).then_inc(s.dx0, 16)
+    act.dma_start(T.ab[:, 0:512], T.a[:, 0:512]).then_inc(s.da0, 16)
+    sy.dma_start(T.xs[:, 1024:2048], T.x[:, 1024:2048]).then_inc(s.dx1, 16)
+    act.dma_start(T.ab[:, 512:1024], T.a[:, 512:1024]).then_inc(s.da1, 16)
+    sy.dma_start(T.ab[:, 1024:2048], T.a[:, 1024:2048]).then_inc(s.da2, 16)
+    act.dma_start(T.uv[:, 0:512], T.u[:]).then_inc(s.du, 16)
+    sy.dma_start(T.uv[:, 512:1024], T.v[:]).then_inc(s.dv, 16)
+
+    e_iota = done(g.iota(T.pidx[:], [[0, 1]], 0, 1), "sg")
+
+    e = V(v.memset(T.mk[:], 1.0))
+    e2 = V(v.memset(T.mi[:], 1.0))
+    V(v.memset(T.tb[:, 0:4 * W:W], 0.0))
+    e3 = V(v.memset(T.zus[:, SL:SL + 8], 0.0))
+    vw(e)
+    for n, k in enumerate(LV):
+        V(v.memset(T.mk[:, X * n:X * n + X:1 << k], 0.0))
+    vw(e2)
+    e_mk = V(v.memset(T.mi[:, 0:2 * SL:2], 0.0))
+    vw(e_iota)
+    e_pid = V(v.tensor_scalar(T.pid16[:], T.pidx[:], 15, None, A.bitwise_and))
+    need(g, "g", e_pid)
+    for n, tab in enumerate((T.pf, T.pg)):
+        g.indirect_dma_start(T.pp[:, 16 * n:16 * n + 16], None, tab[:], IndirectOffsetOnAxis(ap=T.pid16[:, 0:1], axis=0),
+                             bounds_check=15).then_inc(s.gi, 16)
+
+    vw(("dlo", 16), ("dln", 16))
+    m = 6 * ((q + 1) % N)
+    runs = [(0, m, 24)] + ([(24 - m, 0, m)] if m else [])
+    for d, a, b in runs:
+        V(v.tensor_copy(T.wt[:, 1, 0, 0, d:d + b - a], T.lob[:, a:b]))
+        e = V(v.tensor_tensor(T.wt[:, 0, 0, 0, d:d + b - a], T.lnb[:, a:b], T.lob[:, a:b], A.add))
+    vw(e)
+    V(v.tensor_scalar(T.wt[:, 1, 1, 0], T.wt[:, 1, 0, 0], -1, None, A.add))
+    e = V(v.tensor_scalar(T.wt[:, 0, 1, 0], T.wt[:, 0, 0, 0], -1, None, A.add))
+    V(v.tensor_scalar(T.cc[:, 0], T.wt[:, 1, 0, 0], 1.0 / X, float(H0), A.mult, A.add))
+    vw(e)
+    for n in range(1, 5):
+        e = V(v.tensor_scalar(T.wt[:, :, :, n], T.wt[:, :, :, 0], 2 * n, None, A.arith_shift_right))
+    V(v.tensor_scalar(T.cc[:, 1], T.wt[:, 0, 1, 0], -1.0 / X, -float(H0), A.mult, A.add))
+    vw(e)
+    V(v.tensor_tensor(T.vt[:], T.wt[:, 0, :, 1:4], T.wt[:, 1, :, 1:4], A.is_gt))
+    e = V(v.tensor_tensor(T.dd[:], T.wt[:, 0, 1, 1:5], T.wt[:, 1, 0, 1:5], A.subtract))
+    vw(e)
+    for n in range(3):
+        e = V(v.tensor_tensor(T.cc[:], T.cc[:], T.vt[:, :, n], A.add))
+        vw(e)
+    for b in (0, 1):
+        e = V(v.tensor_tensor(T.cc[:, b], T.cc[:, b], T.dd[:, 3], A.add))
+    vw(e)
+    V(v.tensor_scalar(T.offl[:], T.cc[:, 0], float(X), None, A.mult))
+    V(v.tensor_scalar(T.offr[:], T.cc[:, 1], -float(X), None, A.mult))
+
+    def middle():
+        V(v.tensor_scalar(T.eq[:], T.dd[:, 1:4], 0.0, None, A.is_equal))
+        V(v.tensor_scalar(T.qq[:], T.dd[:, 0:3], 2.0, None, A.is_ge))
+        e = V(v.tensor_scalar(T.mx[:], T.dd[:, 0:3], 3.0, float(MT * X), A.is_ge, A.mult))
+        for n, k in enumerate(LV):
+            e1 = V(v.tensor_scalar(T.mb[:, n], T.wt[:, 0, 1, n + 1], float(1 << k), float(X * PT[k] - 1), A.mult, A.add))
+        vw(e)
+        e = V(v.tensor_tensor(T.qq[:], T.qq[:], T.eq[:], A.mult))
+        vw(e1)
+        e1 = V(v.tensor_tensor(T.mb[:], T.mb[:], T.mx[:], A.add))
+        vw(e1)
+        e = V(v.tensor_tensor(T.mb[:], T.mb[:], T.qq[:], A.mult))
+        vw(e)
+        e = V(v.tensor_tensor(T.mx[:, 0], T.mb[:, 0], T.mb[:, 1], A.add))
+        vw(e)
+        e = V(v.tensor_tensor(T.mx[:, 1], T.mx[:, 0], T.mb[:, 2], A.add))
+        vw(e)
+        return V(v.tensor_copy(T.offm[:], T.mx[:, 1]))
+
+    def quant(dst, sc, src):
+        return V(v.quantize_mx(dst, sc, src))
+
+    def mm(bank, n, w, wc, x, xc):
+        return done(ten.matmul_mx(T.ps[:, 512 * bank:512 * bank + n], w, wc, x, xc, True, True), "st")
+
+    def col(i, t, a=0, b=X, st=1):
+        o = W * i + X * t
+        return T.tb[:, o + a:o + b:st]
+
+    def back(i, t, a, b):
+        o = W * i + X * t
+        return T.tb[:, o + b - 1:(o + a - 1 if o + a else None):-1]
+
+    def relu(i, a, b, bank):
+        return done(act.activation(col(i, H0, a, b), T.ps[:, 512 * bank:512 * bank + b - a], F.Relu, scale=0.05), "sa")
+
+    def prod_z(i, c0, c1, bank):
+        return mm(bank, c1 - c0, T.aq[:, 128 * i:128 * i + 128], T.ac[:, 128 * i:128 * i + 128], T.xq[:, c0:c1], T.xc[:, c0:c1])
+
+    vw(("da0", 16))
+    quant(T.aq[:, 0:128], T.ac[:, 0:128], T.ab[:, 0:512])
+    vw(("dx0", 16))
+    e = quant(T.xq[:, 0:256], T.xc[:, 0:256], T.xs[:, 0:1024])
+    need(ten, "t", e)
+    z = prod_z(0, 0, 256, 0)
+    need(act, "a", z)
+    relu(0, 0, 256, 0)
+    vw(("dx1", 16))
+    e = quant(T.xq[:, 256:512], T.xc[:, 256:512], T.xs[:, 1024:2048])
+    need(ten, "t", e)
+    z = prod_z(0, 256, 512, 1)
+    need(act, "a", z)
+    ev = {0: relu(0, 256, 512, 1)}
+    e_off = middle()
+
+    def more_a():
+        vw(("da1", 16))
+        e = quant(T.aq[:, 128:256], T.ac[:, 128:256], T.ab[:, 512:1024])
+        need(ten, "t", e)
+        z = prod_z(1, 0, 512, 2)
+        need(act, "a", z)
+        ev[1] = relu(1, 0, 512, 2)
+
+    def rest_a():
+        vw(("da2", 16))
+        e = quant(T.aq[:, 256:512], T.ac[:, 256:512], T.ab[:, 1024:2048])
+        need(ten, "t", e)
+        for i in (2, 3):
+            z = prod_z(i, 0, 512, i + 1)
+            need(act, "a", z)
+            ev[i] = relu(i, 0, 512, i + 1)
+
+    def tables(i, hooks):
+        vw(e_mk, ev[i])
+        h = back(i, H0, 0, 256)
+        V(v.tensor_tensor_scan(back(i, SB, 0, 256), h, h, 0.0, A.max, A.max))
+        h = col(i, H0, 256, X)
+        e = V(v.tensor_tensor_scan(col(i, PB, 256, X), h, h, 0.0, A.max, A.max))
+        for n, k in enumerate(LV):
+            mk = T.mk[:, X * n:X * n + X]
+            V(v.tensor_tensor_scan(col(i, PT[k]), mk, col(i, H0), 0.0, A.mult, A.max))
+            e = V(v.tensor_tensor_scan(back(i, ST[k], 0, X), mk, back(i, H0, 0, X), 0.0, A.mult, A.max))
+            if hooks[n]:
+                hooks[n]()
+        vw(e)
+        for k in LV:
+            b = 1 << k
+            e = V(v.tensor_tensor(col(i, MT + PT[k], 3 * b - 1, X, 4 * b), col(i, PT[k], 2 * b - 1, X, 4 * b),
+                                  col(i, PT[k], 3 * b - 1, X, 4 * b), A.max))
+        return e
+
+    def win(i):
+        return T.tb[:, W * i:W * i + W]
+
+    def gather(i, c0, c1, after):
+        need(act, "a", after, e_off)
+        o = 2 * SL * i
+        for n, off in enumerate((T.offl, T.offm)):
+            e = done(act.activation(T.ga[:, o + 2 * c0 + n:o + 2 * c1:2], win(i).indirect(off[:, c0 // 16:c1 // 16]), F.Copy), "sa")
+        return e
+
+    def comb(i, c0, c1, e):
+        vw(e)
+        o = 2 * SL * i
+        e = V(v.tensor_tensor_scan(T.gb[:, o + 2 * c0:o + 2 * c1], T.mi[:, 2 * c0:2 * c1], T.ga[:, o + 2 * c0:o + 2 * c1], 0.0, A.mult, A.max))
+        vw(e)
+        return V(v.tensor_tensor(T.t[:, 4 * c0 + i:4 * c1:4], win(i).indirect(T.offr[:, c0 // 16:c1 // 16]),
+                                 T.gb[:, o + 2 * c0 + 1:o + 2 * c1:2], A.max))
+
+    e0 = tables(0, (more_a, rest_a, None))
+    ga0 = gather(0, 0, SL, e0)
+    e1 = tables(1, (None, None, None))
+    ga1 = gather(1, 0, SL, e1)
+    comb(0, 0, SL, ga0)
+    e2 = tables(2, (None, None, None))
+    ga2 = gather(2, 0, SL, e2)
+    comb(1, 0, SL, ga1)
+    e = tables(3, (None, None, None))
+    cuts = ((0, 192), (192, 288), (288, SL))
+    ga3 = [gather(3, c0, c1, e) for c0, c1 in cuts]
+    comb(2, 0, SL, ga2)
+
+    def dst(r):
+        rid, pnc, _ = topo.addr(T.cores[r])
+        return DstId(rid=rid, pnc=pnc)
+
+    def send(js, sq, sc, c0, sem):
+        for kind in (0, 1):
+            tr = []
+            for n, j in enumerate(js):
+                r = (q + 1 + j) % N
+                eng = topo.engines(core, T.cores[r])
+                w = len(eng) // len(js)
+                m = sum(1 << x for x in eng[n * w:n * w + w])
+                a, b, at = c0 + n * CAPP, c0 + (n + 1) * CAPP, CAPP * (2 - j)
+                if kind == 0:
+                    sa, da = sq[:, a:b].bitcast(dt.uint8), T.rq[:, at:at + CAPP].bitcast(dt.uint8)
+                else:
+                    sa, da = sc[:, a:b], T.rc[:, at:at + CAPP]
+                tr.append(RemoteDMATransfer(dst_ids=[dst(r)], dma_engine_mask=m, remote_sem=sem, src=sa, dst=da))
+            g.remote_dma_fused(tr, local_sem=s.loc)
+
+    e = comb(3, *cuts[0], ga3[0])
+    vw(e)
+    e = quant(T.tq[:], T.tc[:], T.t[:, 0:768])
+    need(g, "g", e)
+    send([0, 1], T.tq, T.tc, 0, s.arre)
+    e = comb(3, *cuts[1], ga3[1])
+    vw(e)
+    e = quant(T.tq1[:], T.tc1[:], T.t[:, 640:1152])
+    need(g, "g", e)
+    send([2], T.tq1, T.tc1, 32, s.arrl)
+    e = comb(3, *cuts[2], ga3[2])
+    vw(e)
+    e_own = quant(T.tq2[:], T.tc2[:], T.t[:, 1024:1536])
+    vw(("du", 16), ("dv", 16))
+    e_uv = quant(T.uvq[:], T.uvc[:], T.uv[:])
+
+    c1 = CAPP * (q + 1)
+    vw(("gi", 32))
+    V(v.tensor_scalar(T.pn[:], T.pp[:, 16:32], 0, 1 + c1, A.is_lt, A.mult))
+    e = V(v.tensor_scalar(T.pw[:], T.pp[:], c1, SL, A.is_lt, A.mult))
+    vw(e)
+    e = V(v.tensor_tensor(T.pw[:], T.pw[:], T.pp[:], A.add))
+    vw(e)
+    e_f = V(v.tensor_scalar(T.offf[:], T.pw[:, 0:16], -c1, None, A.add))
+    e = V(v.tensor_tensor(T.pn[:], T.pn[:], T.pw[:, 16:32], A.add))
+    vw(e)
+    e_g = V(v.tensor_scalar(T.offg[:], T.pn[:], -c1, None, A.add))
+
+    def prod(x, xc, n, skip, m, at, bv, bu):
+        ev_ = mm(bv, n, T.uvq[:, 128:256], T.uvc[:, 128:256], x, xc)
+        eu = mm(bu, n, T.uvq[:, 0:128], T.uvc[:, 0:128], x, xc)
+        need(act, "a", ev_)
+        a = done(act.activation(T.zvs[:, at:at + m], T.ps[:, 512 * bv + skip:512 * bv + skip + m], F.Copy), "sa")
+        vw(eu)
+        b = V(v.tensor_copy(T.zus[:, at:at + m], T.ps[:, 512 * bu + skip:512 * bu + skip + m]))
+        return a, b
+
+    need(ten, "t", e_own, e_uv)
+    prod(T.tq2[:], T.tc2[:], 128, 32, CAPP, 288, 5, 6)
+    need(ten, "t", ("arre", 16), ev[3])
+    prod(T.rq[:, 96:288], T.rc[:, 96:288], 192, 0, 192, 96, 7, 0)
+    need(ten, "t", ("arrl", 16))
+    a, b = prod(T.rq[:, 0:128], T.rc[:, 0:128], 128, 0, CAPP, 0, 1, 2)
+    need(act, "a", a, e_f)
+    a = done(act.activation(T.y1[:], T.zvs[:].indirect(T.offf[:]), F.Copy), "sa")
+    vw(a, b, e_g, e3)
+    e = V(v.tensor_tensor(T.ys[:], T.zus[:].indirect(T.offg[:]), T.y1[:], A.add))
+    need(sy, "s", e)
+    sy.dma_start(T.y[:], T.ys[:]).then_inc(s.dy, 16)
+    sy.wait_ge(s.dy, 16)
+    g.wait_ge(s.loc, 32)
+    for name in ("sv", "st", "sa", "sg"):
+        need(g, "g", (name, cnt[name]))

@@ -14,6 +14,7 @@ ST = {2: 5, 4: 6, 6: 7}
 MT = 8
 H0, PB, SB, NT = 4, 0, 8, 12
 W = NT * X
+CUTS = ((0, 2 * CAPP), (2 * CAPP, 3 * CAPP), (3 * CAPP, SL))
 
 SCRATCH = {
     "xs": ("sbuf", [128, 2048], "bfloat16"),
@@ -29,6 +30,8 @@ SCRATCH = {
     "tb": ("sbuf", [128, 4 * W], "bfloat16"),
     "mk": ("sbuf", [128, 3 * X], "bfloat16"),
     "mi": ("sbuf", [128, 2 * SL], "bfloat16"),
+    "one": ("sbuf", [128, 3 * SL], "bfloat16"),
+    "m3": ("sbuf", [128, 3 * SL], "bfloat16"),
     "lnb": ("sbuf", [128, 24], "int32"),
     "lob": ("sbuf", [128, 24], "int32"),
     "wt": ("sbuf", [128, 2, 2, 5, 24], "int32"),
@@ -42,8 +45,8 @@ SCRATCH = {
     "offl": ("sbuf", [128, 24], "uint16"),
     "offr": ("sbuf", [128, 24], "uint16"),
     "offm": ("sbuf", [128, 24], "uint16"),
-    "ga": ("sbuf", [128, 8 * SL], "bfloat16"),
-    "gb": ("sbuf", [128, 8 * SL], "bfloat16"),
+    "ga": ("sbuf", [128, 12 * SL], "bfloat16"),
+    "gb": ("sbuf", [128, 12 * SL], "bfloat16"),
     "t": ("sbuf", [128, 4 * SL], "bfloat16"),
     "tq": ("sbuf", [128, 192], "float8_e4m3fn_x4"),
     "tc": ("sbuf", [128, 192], "uint8"),
@@ -105,16 +108,17 @@ def rank_program(g, core, T, topo):
     sy.dma_start(T.uv[:, 512:1024], T.v[:]).then_inc(s.dv, 16)
 
     e_iota = done(g.iota(T.pidx[:], [[0, 1]], 0, 1), "sg")
+    done(g.iota(T.mi[:], [[0, SL], [1, 2]], 0, 0, allow_small_or_imprecise_dtypes=True), "sg")
+    e = done(g.iota(T.one[:], [[0, 3 * SL]], 1, 0, allow_small_or_imprecise_dtypes=True), "sg")
+    need(g, "g", e)
+    e_mi = done(g.affine_select(T.m3[:], T.one[:], [[0, SL], [1, 3]], A.not_equal, 0.0, 0, 0), "sg")
 
     e = V(v.memset(T.mk[:], 1.0))
-    e2 = V(v.memset(T.mi[:], 1.0))
     V(v.memset(T.tb[:, 0:4 * W:W], 0.0))
     e3 = V(v.memset(T.zus[:, SL:SL + 8], 0.0))
     vw(e)
     for n, k in enumerate(LV):
-        V(v.memset(T.mk[:, X * n:X * n + X:1 << k], 0.0))
-    vw(e2)
-    e_mk = V(v.memset(T.mi[:, 0:2 * SL:2], 0.0))
+        e_mk = V(v.memset(T.mk[:, X * n:X * n + X:1 << k], 0.0))
     vw(e_iota)
     e_pid = V(v.tensor_scalar(T.pid16[:], T.pidx[:], 15, None, A.bitwise_and))
     need(g, "g", e_pid)
@@ -131,35 +135,39 @@ def rank_program(g, core, T, topo):
     vw(e)
     V(v.tensor_scalar(T.wt[:, 1, 1, 0], T.wt[:, 1, 0, 0], -1, None, A.add))
     e = V(v.tensor_scalar(T.wt[:, 0, 1, 0], T.wt[:, 0, 0, 0], -1, None, A.add))
-    V(v.tensor_scalar(T.cc[:, 0], T.wt[:, 1, 0, 0], 1.0 / X, float(H0), A.mult, A.add))
+    V(v.tensor_scalar(T.cc[:, 0], T.wt[:, 1, 0, 0], 1.0 / X, None, A.mult))
     vw(e)
     for n in range(1, 5):
         e = V(v.tensor_scalar(T.wt[:, :, :, n], T.wt[:, :, :, 0], 2 * n, None, A.arith_shift_right))
     V(v.tensor_scalar(T.cc[:, 1], T.wt[:, 0, 1, 0], -1.0 / X, -float(H0), A.mult, A.add))
     vw(e)
     V(v.tensor_tensor(T.vt[:], T.wt[:, 0, :, 1:4], T.wt[:, 1, :, 1:4], A.is_gt))
-    e = V(v.tensor_tensor(T.dd[:], T.wt[:, 0, 1, 1:5], T.wt[:, 1, 0, 1:5], A.subtract))
-    vw(e)
+    e_dd = V(v.tensor_tensor(T.dd[:], T.wt[:, 0, 1, 1:5], T.wt[:, 1, 0, 1:5], A.subtract))
+    vw(e_dd)
     for n in range(3):
-        e = V(v.tensor_tensor(T.cc[:], T.cc[:], T.vt[:, :, n], A.add))
-        vw(e)
-    for b in (0, 1):
-        e = V(v.tensor_tensor(T.cc[:, b], T.cc[:, b], T.dd[:, 3], A.add))
-    vw(e)
-    V(v.tensor_scalar(T.offl[:], T.cc[:, 0], float(X), None, A.mult))
-    V(v.tensor_scalar(T.offr[:], T.cc[:, 1], -float(X), None, A.mult))
+        e_cc = V(v.tensor_tensor(T.cc[:], T.cc[:], T.vt[:, :, n], A.add))
+        vw(e_cc)
 
-    def middle():
+    def ends():
+        for b in (0, 1):
+            e = V(v.tensor_tensor(T.cc[:, b], T.cc[:, b], T.dd[:, 3], A.add))
+        vw(e)
+        V(v.tensor_scalar(T.offl[:], T.cc[:, 0], float(X), None, A.mult))
+        V(v.tensor_scalar(T.offr[:], T.cc[:, 1], -float(X), None, A.mult))
+
+    def middle_a():
         V(v.tensor_scalar(T.eq[:], T.dd[:, 1:4], 0.0, None, A.is_equal))
         V(v.tensor_scalar(T.qq[:], T.dd[:, 0:3], 2.0, None, A.is_ge))
         e = V(v.tensor_scalar(T.mx[:], T.dd[:, 0:3], 3.0, float(MT * X), A.is_ge, A.mult))
         for n, k in enumerate(LV):
-            e1 = V(v.tensor_scalar(T.mb[:, n], T.wt[:, 0, 1, n + 1], float(1 << k), float(X * PT[k] - 1), A.mult, A.add))
+            e = V(v.tensor_scalar(T.mb[:, n], T.wt[:, 0, 1, n + 1], float(1 << k), float(X * PT[k] - 1), A.mult, A.add))
+        return e
+
+    def middle_b(e):
         vw(e)
-        e = V(v.tensor_tensor(T.qq[:], T.qq[:], T.eq[:], A.mult))
-        vw(e1)
-        e1 = V(v.tensor_tensor(T.mb[:], T.mb[:], T.mx[:], A.add))
-        vw(e1)
+        V(v.tensor_tensor(T.qq[:], T.qq[:], T.eq[:], A.mult))
+        e = V(v.tensor_tensor(T.mb[:], T.mb[:], T.mx[:], A.add))
+        vw(e)
         e = V(v.tensor_tensor(T.mb[:], T.mb[:], T.qq[:], A.mult))
         vw(e)
         e = V(v.tensor_tensor(T.mx[:, 0], T.mb[:, 0], T.mb[:, 1], A.add))
@@ -195,14 +203,10 @@ def rank_program(g, core, T, topo):
     need(ten, "t", e)
     z = prod_z(0, 0, 256, 0)
     need(act, "a", z)
-    relu(0, 0, 256, 0)
-    vw(("dx1", 16))
-    e = quant(T.xq[:, 256:512], T.xc[:, 256:512], T.xs[:, 1024:2048])
-    need(ten, "t", e)
-    z = prod_z(0, 256, 512, 1)
-    need(act, "a", z)
-    ev = {0: relu(0, 256, 512, 1)}
-    e_off = middle()
+    eh0 = relu(0, 0, 256, 0)
+    ends()
+    em = middle_a()
+    ev = {}
 
     def more_a():
         vw(("da1", 16))
@@ -221,18 +225,27 @@ def rank_program(g, core, T, topo):
             need(act, "a", z)
             ev[i] = relu(i, 0, 512, i + 1)
 
-    def tables(i, hooks):
-        vw(e_mk, ev[i])
-        h = back(i, H0, 0, 256)
-        V(v.tensor_tensor_scan(back(i, SB, 0, 256), h, h, 0.0, A.max, A.max))
-        h = col(i, H0, 256, X)
-        e = V(v.tensor_tensor_scan(col(i, PB, 256, X), h, h, 0.0, A.max, A.max))
+    def scans_s(i, a, b, hooks=()):
+        if a == 0:
+            h = back(i, H0, 0, 256)
+            e = V(v.tensor_tensor_scan(back(i, SB, 0, 256), h, h, 0.0, A.max, A.max))
         for n, k in enumerate(LV):
-            mk = T.mk[:, X * n:X * n + X]
-            V(v.tensor_tensor_scan(col(i, PT[k]), mk, col(i, H0), 0.0, A.mult, A.max))
-            e = V(v.tensor_tensor_scan(back(i, ST[k], 0, X), mk, back(i, H0, 0, X), 0.0, A.mult, A.max))
-            if hooks[n]:
+            e = V(v.tensor_tensor_scan(back(i, ST[k], a, b), T.mk[:, X * n:X * n + b - a], back(i, H0, a, b), 0.0, A.mult, A.max))
+            if n < len(hooks) and hooks[n]:
                 hooks[n]()
+        return e
+
+    def scans_p(i, a, b, hooks=()):
+        if b == X:
+            h = col(i, H0, 256, X)
+            e = V(v.tensor_tensor_scan(col(i, PB, 256, X), h, h, 0.0, A.max, A.max))
+        for n, k in enumerate(LV):
+            e = V(v.tensor_tensor_scan(col(i, PT[k], a, b), T.mk[:, X * n:X * n + b - a], col(i, H0, a, b), 0.0, A.mult, A.max))
+            if n < len(hooks) and hooks[n]:
+                hooks[n]()
+        return e
+
+    def middles(i, e):
         vw(e)
         for k in LV:
             b = 1 << k
@@ -240,36 +253,69 @@ def rank_program(g, core, T, topo):
                                   col(i, PT[k], 3 * b - 1, X, 4 * b), A.max))
         return e
 
-    def win(i):
-        return T.tb[:, W * i:W * i + W]
+    def win(i, a, b):
+        return T.tb[:, W * i + X * a:W * i + X * b]
 
-    def gather(i, c0, c1, after):
-        need(act, "a", after, e_off)
-        o = 2 * SL * i
-        for n, off in enumerate((T.offl, T.offm)):
-            e = done(act.activation(T.ga[:, o + 2 * c0 + n:o + 2 * c1:2], win(i).indirect(off[:, c0 // 16:c1 // 16]), F.Copy), "sa")
+    def gather(i, c0, c1, after, ns, w):
+        o = 3 * SL * i
+        for n in ns:
+            off, a, b = ((T.offl, H0, SB + 1), (T.offm, 0, NT), (T.offr, 0, H0 + 1))[n]
+            need(act, "a", after, e_off)
+            e = done(act.activation(T.ga[:, o + w * c0 + n:o + w * c1:w], win(i, a, b).indirect(off[:, c0 // 16:c1 // 16]), F.Copy), "sa")
         return e
 
-    def comb(i, c0, c1, e):
+    def largest(i, c0, c1, w, mk, e):
+        vw(e, e_mi)
+        o = 3 * SL * i
+        return V(v.tensor_tensor_scan(T.gb[:, o + w * c0:o + w * c1], mk[:, w * c0:w * c1], T.ga[:, o + w * c0:o + w * c1], 0.0, A.mult, A.max))
+
+    def comb2(i, c0, c1, e):
+        e = largest(i, c0, c1, 2, T.mi, e)
         vw(e)
-        o = 2 * SL * i
-        e = V(v.tensor_tensor_scan(T.gb[:, o + 2 * c0:o + 2 * c1], T.mi[:, 2 * c0:2 * c1], T.ga[:, o + 2 * c0:o + 2 * c1], 0.0, A.mult, A.max))
-        vw(e)
-        return V(v.tensor_tensor(T.t[:, 4 * c0 + i:4 * c1:4], win(i).indirect(T.offr[:, c0 // 16:c1 // 16]),
+        o = 3 * SL * i
+        return V(v.tensor_tensor(T.t[:, 4 * c0 + i:4 * c1:4], win(i, 0, H0 + 1).indirect(T.offr[:, c0 // 16:c1 // 16]),
                                  T.gb[:, o + 2 * c0 + 1:o + 2 * c1:2], A.max))
 
-    e0 = tables(0, (more_a, rest_a, None))
-    ga0 = gather(0, 0, SL, e0)
-    e1 = tables(1, (None, None, None))
-    ga1 = gather(1, 0, SL, e1)
-    comb(0, 0, SL, ga0)
-    e2 = tables(2, (None, None, None))
-    ga2 = gather(2, 0, SL, e2)
-    comb(1, 0, SL, ga1)
-    e = tables(3, (None, None, None))
-    cuts = ((0, 192), (192, 288), (288, SL))
-    ga3 = [gather(3, c0, c1, e) for c0, c1 in cuts]
-    comb(2, 0, SL, ga2)
+    def take3(i, e):
+        need(act, "a", e)
+        o = 3 * SL * i
+        return done(act.activation(T.t[:, i:4 * SL:4], T.gb[:, o + 2:o + 3 * SL:3], F.Copy), "sa")
+
+    vw(e_mk, eh0)
+    scans_s(0, 0, 256)
+    scans_p(0, 0, 256)
+    vw(("dx1", 16))
+    e = quant(T.xq[:, 256:512], T.xc[:, 256:512], T.xs[:, 1024:2048])
+    need(ten, "t", e)
+    z = prod_z(0, 256, 512, 1)
+    need(act, "a", z)
+    ev[0] = relu(0, 256, 512, 1)
+    e_off = middle_b(em)
+    vw(ev[0])
+    gather(0, 0, SL, scans_s(0, 256, X, (None, more_a)), (0,), 3)
+    ga0 = gather(0, 0, SL, middles(0, scans_p(0, 256, X, (None, rest_a))), (1, 2), 3)
+    vw(ev[1])
+    gather(1, 0, SL, scans_s(1, 0, X), (0,), 3)
+    ga1 = gather(1, 0, SL, middles(1, scans_p(1, 0, X)), (1, 2), 3)
+    vw(ev[2])
+    gather(2, *CUTS[0], scans_s(2, 0, X), (0,), 2)
+    e2 = middles(2, scans_p(2, 0, X))
+    l0 = largest(0, 0, SL, 3, T.m3, ga0)
+    ga2 = [gather(2, *CUTS[0], e2, (1,), 2)]
+    vw(ev[3])
+    gather(3, *CUTS[0], scans_s(3, 0, X), (0,), 2)
+    take3(0, l0)
+    l1 = []
+    e = middles(3, scans_p(3, 0, X, (None, lambda: l1.append(largest(1, 0, SL, 3, T.m3, ga1)))))
+    ga3 = [gather(3, *CUTS[0], e, (1,), 2)]
+    e_t = take3(1, l1[0])
+    for c in CUTS[1:]:
+        ga2.append(gather(2, *c, e2, (0, 1), 2))
+        ga3.append(gather(3, *c, e, (0, 1), 2))
+
+    def pieces(n):
+        comb2(2, *CUTS[n], ga2[n])
+        vw(comb2(3, *CUTS[n], ga3[n]), e_t)
 
     def dst(r):
         rid, pnc, _ = topo.addr(T.cores[r])
@@ -291,18 +337,15 @@ def rank_program(g, core, T, topo):
                 tr.append(RemoteDMATransfer(dst_ids=[dst(r)], dma_engine_mask=m, remote_sem=sem, src=sa, dst=da))
             g.remote_dma_fused(tr, local_sem=s.loc)
 
-    e = comb(3, *cuts[0], ga3[0])
-    vw(e)
+    pieces(0)
     e = quant(T.tq[:], T.tc[:], T.t[:, 0:768])
     need(g, "g", e)
     send([0, 1], T.tq, T.tc, 0, s.arre)
-    e = comb(3, *cuts[1], ga3[1])
-    vw(e)
+    pieces(1)
     e = quant(T.tq1[:], T.tc1[:], T.t[:, 640:1152])
     need(g, "g", e)
     send([2], T.tq1, T.tc1, 32, s.arrl)
-    e = comb(3, *cuts[2], ga3[2])
-    vw(e)
+    pieces(2)
     e_own = quant(T.tq2[:], T.tc2[:], T.t[:, 1024:1536])
     vw(("du", 16), ("dv", 16))
     e_uv = quant(T.uvq[:], T.uvc[:], T.uv[:])
@@ -335,12 +378,15 @@ def rank_program(g, core, T, topo):
     need(ten, "t", ("arrl", 16))
     a, b = prod(T.rq[:, 0:128], T.rc[:, 0:128], 128, 0, CAPP, 0, 1, 2)
     need(act, "a", a, e_f)
-    a = done(act.activation(T.y1[:], T.zvs[:].indirect(T.offf[:]), F.Copy), "sa")
-    vw(a, b, e_g, e3)
-    e = V(v.tensor_tensor(T.ys[:], T.zus[:].indirect(T.offg[:]), T.y1[:], A.add))
-    need(sy, "s", e)
-    sy.dma_start(T.y[:], T.ys[:]).then_inc(s.dy, 16)
-    sy.wait_ge(s.dy, 16)
+    H = P // 2
+    a = [done(act.activation(T.y1[:, c:c + H], T.zvs[:].indirect(T.offf[:, c // 16:(c + H) // 16]), F.Copy), "sa") for c in (0, H)]
+    vw(b, e_g, e3)
+    for n, c in enumerate((0, H)):
+        vw(a[n])
+        e = V(v.tensor_tensor(T.ys[:, c:c + H], T.zus[:].indirect(T.offg[:, c // 16:(c + H) // 16]), T.y1[:, c:c + H], A.add))
+        need(sy, "s", e)
+        sy.dma_start(T.y[:, c:c + H], T.ys[:, c:c + H]).then_inc(s.dy, 16)
+    sy.wait_ge(s.dy, 32)
     g.wait_ge(s.loc, 32)
     for name in ("sv", "st", "sa", "sg"):
         need(g, "g", (name, cnt[name]))

@@ -8,13 +8,17 @@ CAPP = 96
 P = 256
 SL = N * CAPP
 X = 512
-LV = (2, 4, 6)
-PT = {2: 3, 4: 2, 6: 1}
-ST = {2: 5, 4: 6, 6: 7}
-MT = 8
-H0, PB, SB, NT = 4, 0, 8, 12
-W = NT * X
+LV = (2, 4)
+P16, P4, H0, S4, S16, NT = 0, 1, 2, 3, 4, 5
+PT = (P4, P16)
+ST = (S4, S16)
+NB = X // 16
+RW = 2 * NB
+NR = 35
+CROW = 32
+LEFT, MID, RIGHT = 0, 1, 2
 CUTS = ((0, 2 * CAPP), (2 * CAPP, 3 * CAPP), (3 * CAPP, SL))
+ALL, EARLY, REST = (0, SL), CUTS[0], (2 * CAPP, SL)
 
 SCRATCH = {
     "xs": ("sbuf", [128, 2048], "bfloat16"),
@@ -27,21 +31,25 @@ SCRATCH = {
     "uvq": ("sbuf", [128, 256], "float8_e4m3fn_x4"),
     "uvc": ("sbuf", [128, 256], "uint8"),
     "ps": ("psum", [128, 4096], "float32"),
-    "tb": ("sbuf", [128, 4 * W], "bfloat16"),
-    "mk": ("sbuf", [128, 3 * X], "bfloat16"),
+    "tw": ("sbuf", [128, 4 * NT * X], "bfloat16"),
+    "bm": ("sbuf", [128, 4 * RW], "bfloat16"),
+    "bt": ("sbuf", [128, 2 * NR * RW], "bfloat16"),
+    "mk": ("sbuf", [128, 2 * X], "bfloat16"),
+    "mz": ("sbuf", [128, 5 * NB], "bfloat16"),
     "mi": ("sbuf", [128, 2 * SL], "bfloat16"),
     "one": ("sbuf", [128, 3 * SL], "bfloat16"),
     "m3": ("sbuf", [128, 3 * SL], "bfloat16"),
     "lnb": ("sbuf", [128, 24], "int32"),
     "lob": ("sbuf", [128, 24], "int32"),
-    "wt": ("sbuf", [128, 2, 2, 5, 24], "int32"),
-    "vt": ("sbuf", [128, 2, 3, 24], "float32"),
-    "dd": ("sbuf", [128, 4, 24], "float32"),
+    "wt": ("sbuf", [128, 2, 2, 3, 24], "int32"),
+    "vt": ("sbuf", [128, 2, 2, 24], "float32"),
+    "dd": ("sbuf", [128, 2, 24], "float32"),
     "cc": ("sbuf", [128, 2, 24], "float32"),
-    "eq": ("sbuf", [128, 3, 24], "float32"),
-    "qq": ("sbuf", [128, 3, 24], "float32"),
-    "mb": ("sbuf", [128, 3, 24], "float32"),
-    "mx": ("sbuf", [128, 3, 24], "float32"),
+    "eq": ("sbuf", [128, 24], "float32"),
+    "qq": ("sbuf", [128, 2, 24], "float32"),
+    "mb": ("sbuf", [128, 2, 24], "float32"),
+    "mc": ("sbuf", [128, 24], "float32"),
+    "mx": ("sbuf", [128, 24], "float32"),
     "offl": ("sbuf", [128, 24], "uint16"),
     "offr": ("sbuf", [128, 24], "uint16"),
     "offm": ("sbuf", [128, 24], "uint16"),
@@ -94,6 +102,9 @@ def rank_program(g, core, T, topo):
     def V(ins):
         return done(ins, "sv")
 
+    def S(ins):
+        return done(ins, "sa")
+
     def vw(*evs):
         need(v, "v", *evs)
 
@@ -113,12 +124,16 @@ def rank_program(g, core, T, topo):
     need(g, "g", e)
     e_mi = done(g.affine_select(T.m3[:], T.one[:], [[0, SL], [1, 3]], A.not_equal, 0.0, 0, 0), "sg")
 
-    e = V(v.memset(T.mk[:], 1.0))
-    V(v.memset(T.tb[:, 0:4 * W:W], 0.0))
+    V(v.memset(T.mk[:], 1.0))
+    e = V(v.memset(T.mz[:], 1.0))
+    for p in (0, 1):
+        V(v.memset(T.bt[:, NR * RW * p:NR * RW * p + RW], 0.0))
     e3 = V(v.memset(T.zus[:, SL:SL + 8], 0.0))
     vw(e)
     for n, k in enumerate(LV):
-        e_mk = V(v.memset(T.mk[:, X * n:X * n + X:1 << k], 0.0))
+        V(v.memset(T.mk[:, X * n:X * n + X:1 << k], 0.0))
+    V(v.memset(T.mz[:, NB:2 * NB + 1:NB], 0.0))
+    e_mk = V(v.memset(T.mz[:, 3 * NB + 1:4 * NB + 2:NB], 0.0))
     vw(e_iota)
     e_pid = V(v.tensor_scalar(T.pid16[:], T.pidx[:], 15, None, A.bitwise_and))
     need(g, "g", e_pid)
@@ -135,46 +150,44 @@ def rank_program(g, core, T, topo):
     vw(e)
     V(v.tensor_scalar(T.wt[:, 1, 1, 0], T.wt[:, 1, 0, 0], -1, None, A.add))
     e = V(v.tensor_scalar(T.wt[:, 0, 1, 0], T.wt[:, 0, 0, 0], -1, None, A.add))
-    V(v.tensor_scalar(T.cc[:, 0], T.wt[:, 1, 0, 0], 1.0 / X, None, A.mult))
+    V(v.tensor_scalar(T.cc[:, 0], T.wt[:, 1, 0, 0], 0.5 / X, None, A.mult))
     vw(e)
-    for n in range(1, 5):
-        e = V(v.tensor_scalar(T.wt[:, :, :, n], T.wt[:, :, :, 0], 2 * n, None, A.arith_shift_right))
-    V(v.tensor_scalar(T.cc[:, 1], T.wt[:, 0, 1, 0], -1.0 / X, -float(H0), A.mult, A.add))
+    for n, k in enumerate(LV):
+        e = V(v.tensor_scalar(T.wt[:, :, :, n + 1], T.wt[:, :, :, 0], k, None, A.arith_shift_right))
+    V(v.tensor_scalar(T.cc[:, 1], T.wt[:, 0, 1, 0], -0.5 / X, -float(H0), A.mult, A.add))
     vw(e)
-    V(v.tensor_tensor(T.vt[:], T.wt[:, 0, :, 1:4], T.wt[:, 1, :, 1:4], A.is_gt))
-    e_dd = V(v.tensor_tensor(T.dd[:], T.wt[:, 0, 1, 1:5], T.wt[:, 1, 0, 1:5], A.subtract))
+    V(v.tensor_tensor(T.vt[:], T.wt[:, 0, :, 1:3], T.wt[:, 1, :, 1:3], A.is_gt))
+    e_dd = V(v.tensor_tensor(T.dd[:], T.wt[:, 0, 1, 1:3], T.wt[:, 1, 0, 1:3], A.subtract))
     vw(e_dd)
-    for n in range(3):
-        e_cc = V(v.tensor_tensor(T.cc[:], T.cc[:], T.vt[:, :, n], A.add))
-        vw(e_cc)
 
     def ends():
-        for b in (0, 1):
-            e = V(v.tensor_tensor(T.cc[:, b], T.cc[:, b], T.dd[:, 3], A.add))
-        vw(e)
-        V(v.tensor_scalar(T.offl[:], T.cc[:, 0], float(X), None, A.mult))
-        V(v.tensor_scalar(T.offr[:], T.cc[:, 1], -float(X), None, A.mult))
+        for n in (0, 1):
+            e = V(v.tensor_tensor(T.cc[:], T.cc[:], T.vt[:, :, n], A.add))
+            vw(e)
+        V(v.tensor_scalar(T.offl[:], T.cc[:, 0], 2.0 * X, None, A.mult))
+        V(v.tensor_scalar(T.offr[:], T.cc[:, 1], -2.0 * X, None, A.mult))
 
     def middle_a():
-        V(v.tensor_scalar(T.eq[:], T.dd[:, 1:4], 0.0, None, A.is_equal))
-        V(v.tensor_scalar(T.qq[:], T.dd[:, 0:3], 2.0, None, A.is_ge))
-        e = V(v.tensor_scalar(T.mx[:], T.dd[:, 0:3], 3.0, float(MT * X), A.is_ge, A.mult))
-        for n, k in enumerate(LV):
-            e = V(v.tensor_scalar(T.mb[:, n], T.wt[:, 0, 1, n + 1], float(1 << k), float(X * PT[k] - 1), A.mult, A.add))
-        return e
+        V(v.tensor_scalar(T.qq[:], T.dd[:], 2.0, None, A.is_ge))
+        V(v.tensor_scalar(T.eq[:], T.dd[:, 1], 0.0, None, A.is_equal))
+        V(v.tensor_scalar(T.mx[:], T.dd[:, 0], 3.0, float(RW), A.is_ge, A.mult))
+        V(v.tensor_scalar(T.mb[:, 0], T.wt[:, 0, 1, 1], float(RW), float(RW * (CROW - 2)), A.mult, A.add))
+        V(v.tensor_scalar(T.mb[:, 1], T.wt[:, 1, 0, 2], float(RW), float(RW - 1), A.mult, A.add))
+        return V(v.tensor_scalar(T.mc[:], T.wt[:, 0, 1, 2], float(1 - 4 * RW), None, A.mult))
 
     def middle_b(e):
         vw(e)
-        V(v.tensor_tensor(T.qq[:], T.qq[:], T.eq[:], A.mult))
-        e = V(v.tensor_tensor(T.mb[:], T.mb[:], T.mx[:], A.add))
+        V(v.tensor_tensor(T.qq[:, 0], T.qq[:, 0], T.eq[:], A.mult))
+        V(v.tensor_tensor(T.mb[:, 1], T.mb[:, 1], T.wt[:, 0, 1, 2], A.add))
+        e = V(v.tensor_tensor(T.mx[:], T.mx[:], T.mc[:], A.add))
+        vw(e)
+        e = V(v.tensor_tensor(T.mb[:, 0], T.mb[:, 0], T.mx[:], A.add))
         vw(e)
         e = V(v.tensor_tensor(T.mb[:], T.mb[:], T.qq[:], A.mult))
         vw(e)
-        e = V(v.tensor_tensor(T.mx[:, 0], T.mb[:, 0], T.mb[:, 1], A.add))
+        e = V(v.tensor_tensor(T.mx[:], T.mb[:, 0], T.mb[:, 1], A.add))
         vw(e)
-        e = V(v.tensor_tensor(T.mx[:, 1], T.mx[:, 0], T.mb[:, 2], A.add))
-        vw(e)
-        return V(v.tensor_copy(T.offm[:], T.mx[:, 1]))
+        return V(v.tensor_copy(T.offm[:], T.mx[:]))
 
     def quant(dst, sc, src):
         return V(v.quantize_mx(dst, sc, src))
@@ -182,16 +195,19 @@ def rank_program(g, core, T, topo):
     def mm(bank, n, w, wc, x, xc):
         return done(ten.matmul_mx(T.ps[:, 512 * bank:512 * bank + n], w, wc, x, xc, True, True), "st")
 
+    def place(i, t):
+        return X * (2 * (NT * (i // 2) + t) + i % 2)
+
     def col(i, t, a=0, b=X, st=1):
-        o = W * i + X * t
-        return T.tb[:, o + a:o + b:st]
+        o = place(i, t)
+        return T.tw[:, o + a:o + b:st]
 
     def back(i, t, a, b):
-        o = W * i + X * t
-        return T.tb[:, o + b - 1:(o + a - 1 if o + a else None):-1]
+        o = place(i, t)
+        return T.tw[:, o + b - 1:(o + a - 1 if o + a else None):-1]
 
     def relu(i, a, b, bank):
-        return done(act.activation(col(i, H0, a, b), T.ps[:, 512 * bank:512 * bank + b - a], F.Relu, scale=0.05), "sa")
+        return S(act.activation(col(i, H0, a, b), T.ps[:, 512 * bank:512 * bank + b - a], F.Relu, scale=0.05))
 
     def prod_z(i, c0, c1, bank):
         return mm(bank, c1 - c0, T.aq[:, 128 * i:128 * i + 128], T.ac[:, 128 * i:128 * i + 128], T.xq[:, c0:c1], T.xc[:, c0:c1])
@@ -208,114 +224,128 @@ def rank_program(g, core, T, topo):
     em = middle_a()
     ev = {}
 
-    def more_a():
-        vw(("da1", 16))
-        e = quant(T.aq[:, 128:256], T.ac[:, 128:256], T.ab[:, 512:1024])
+    def quant_a(i0, i1, sem):
+        vw((sem, 16))
+        e = quant(T.aq[:, 128 * i0:128 * i1], T.ac[:, 128 * i0:128 * i1], T.ab[:, 512 * i0:512 * i1])
         need(ten, "t", e)
-        z = prod_z(1, 0, 512, 2)
-        need(act, "a", z)
-        ev[1] = relu(1, 0, 512, 2)
-
-    def rest_a():
-        vw(("da2", 16))
-        e = quant(T.aq[:, 256:512], T.ac[:, 256:512], T.ab[:, 1024:2048])
-        need(ten, "t", e)
-        for i in (2, 3):
+        for i in range(i0, i1):
             z = prod_z(i, 0, 512, i + 1)
             need(act, "a", z)
             ev[i] = relu(i, 0, 512, i + 1)
 
-    def scans_s(i, a, b, hooks=()):
-        if a == 0:
-            h = back(i, H0, 0, 256)
-            e = V(v.tensor_tensor_scan(back(i, SB, 0, 256), h, h, 0.0, A.max, A.max))
-        for n, k in enumerate(LV):
-            e = V(v.tensor_tensor_scan(back(i, ST[k], a, b), T.mk[:, X * n:X * n + b - a], back(i, H0, a, b), 0.0, A.mult, A.max))
-            if n < len(hooks) and hooks[n]:
-                hooks[n]()
-        return e
+    def scan_s(i, n, a=0, b=X):
+        return V(v.tensor_tensor_scan(back(i, ST[n], a, b), T.mk[:, X * n:X * n + b - a], back(i, H0, a, b), 0.0, A.mult, A.max))
 
-    def scans_p(i, a, b, hooks=()):
-        if b == X:
-            h = col(i, H0, 256, X)
-            e = V(v.tensor_tensor_scan(col(i, PB, 256, X), h, h, 0.0, A.max, A.max))
-        for n, k in enumerate(LV):
-            e = V(v.tensor_tensor_scan(col(i, PT[k], a, b), T.mk[:, X * n:X * n + b - a], col(i, H0, a, b), 0.0, A.mult, A.max))
-            if n < len(hooks) and hooks[n]:
-                hooks[n]()
-        return e
+    def scan_p(i, n, a=0, b=X):
+        return V(v.tensor_tensor_scan(col(i, PT[n], a, b), T.mk[:, X * n:X * n + b - a], col(i, H0, a, b), 0.0, A.mult, A.max))
 
-    def middles(i, e):
+    def middles(p, e):
+        i, o, b = 2 * p, NR * RW * p, 2 * RW * p
         vw(e)
-        for k in LV:
-            b = 1 << k
-            e = V(v.tensor_tensor(col(i, MT + PT[k], 3 * b - 1, X, 4 * b), col(i, PT[k], 2 * b - 1, X, 4 * b),
-                                  col(i, PT[k], 3 * b - 1, X, 4 * b), A.max))
+        for c in (0, RW):
+            e = V(v.tensor_copy(T.bm[:, b + c:b + c + RW], col(i, P16, 15, 2 * X, 16)))
+        u, w = col(i, P4, 7, 2 * X, 16), col(i, P4, 11, 2 * X, 16)
+        at = o + RW * CROW
+        V(v.tensor_copy(T.bt[:, at:at + RW], u))
+        V(v.tensor_copy(T.bt[:, at + RW:at + 2 * RW], w))
+        V(v.tensor_tensor(T.bt[:, at + 2 * RW:at + 3 * RW], u, w, A.max))
+        vw(e)
+        for r in range(1, NB - 1, 2):
+            e = V(v.tensor_tensor_scan(T.bt[:, o + RW * r:o + RW * (r + 2)], T.mz[:, NB - r:5 * NB - r], T.bm[:, b:b + 2 * RW],
+                                       0.0, A.mult, A.max))
         return e
 
-    def win(i, a, b):
-        return T.tb[:, W * i + X * a:W * i + X * b]
+    def win(i, n):
+        if n == MID:
+            o = NR * RW * (i // 2)
+            return T.bt[:, o + NB * (i % 2):o + NR * RW]
+        a, b = (H0, S16) if n == LEFT else (P16, H0)
+        return T.tw[:, place(i, a):place(i, b) + X]
+
+    def off(n, c0, c1):
+        return (T.offl, T.offm, T.offr)[n][:, c0 // 16:c1 // 16]
 
     def gather(i, c0, c1, after, ns, w):
         o = 3 * SL * i
-        for n in ns:
-            off, a, b = ((T.offl, H0, SB + 1), (T.offm, 0, NT), (T.offr, 0, H0 + 1))[n]
+        for at, n in ns:
             need(act, "a", after, e_off)
-            e = done(act.activation(T.ga[:, o + w * c0 + n:o + w * c1:w], win(i, a, b).indirect(off[:, c0 // 16:c1 // 16]), F.Copy), "sa")
+            e = S(act.activation(T.ga[:, o + w * c0 + at:o + w * c1:w], win(i, n).indirect(off(n, c0, c1)), F.Copy))
         return e
 
-    def largest(i, c0, c1, w, mk, e):
+    def largest(i, c0, c1, w, e):
         vw(e, e_mi)
         o = 3 * SL * i
-        return V(v.tensor_tensor_scan(T.gb[:, o + w * c0:o + w * c1], mk[:, w * c0:w * c1], T.ga[:, o + w * c0:o + w * c1], 0.0, A.mult, A.max))
+        return V(v.tensor_tensor_scan(T.gb[:, o + w * c0:o + w * c1], (T.mi if w == 2 else T.m3)[:, w * c0:w * c1],
+                                      T.ga[:, o + w * c0:o + w * c1], 0.0, A.mult, A.max))
 
-    def comb2(i, c0, c1, e):
-        e = largest(i, c0, c1, 2, T.mi, e)
+    def last(i, c0, c1, w):
+        o = 3 * SL * i
+        return T.gb[:, o + w * c0 + w - 1:o + w * c1:w]
+
+    def piece(i, c0, c1):
+        return T.t[:, 4 * c0 + i:4 * c1:4]
+
+    def take(i, c0, c1, w, e):
         vw(e)
-        o = 3 * SL * i
-        return V(v.tensor_tensor(T.t[:, 4 * c0 + i:4 * c1:4], win(i, 0, H0 + 1).indirect(T.offr[:, c0 // 16:c1 // 16]),
-                                 T.gb[:, o + 2 * c0 + 1:o + 2 * c1:2], A.max))
+        return V(v.tensor_copy(piece(i, c0, c1), last(i, c0, c1, w)))
 
-    def take3(i, e):
-        need(act, "a", e)
-        o = 3 * SL * i
-        return done(act.activation(T.t[:, i:4 * SL:4], T.gb[:, o + 2:o + 3 * SL:3], F.Copy), "sa")
+    def join(i, c0, c1, w, n, e):
+        vw(e, e_off)
+        return V(v.tensor_tensor(piece(i, c0, c1), win(i, n).indirect(off(n, c0, c1)), last(i, c0, c1, w), A.max))
 
     vw(e_mk, eh0)
-    scans_s(0, 0, 256)
-    scans_p(0, 0, 256)
+    for n in (0, 1):
+        scan_p(0, n, 0, 256)
+        scan_s(0, n, 0, 256)
     vw(("dx1", 16))
     e = quant(T.xq[:, 256:512], T.xc[:, 256:512], T.xs[:, 1024:2048])
     need(ten, "t", e)
     z = prod_z(0, 256, 512, 1)
     need(act, "a", z)
     ev[0] = relu(0, 256, 512, 1)
+    quant_a(1, 2, "da1")
     e_off = middle_b(em)
     vw(ev[0])
-    gather(0, 0, SL, scans_s(0, 256, X, (None, more_a)), (0,), 3)
-    ga0 = gather(0, 0, SL, middles(0, scans_p(0, 256, X, (None, rest_a))), (1, 2), 3)
+    for n in (0, 1):
+        scan_s(0, n, 256, X)
+        scan_p(0, n, 256, X)
     vw(ev[1])
-    gather(1, 0, SL, scans_s(1, 0, X), (0,), 3)
-    ga1 = gather(1, 0, SL, middles(1, scans_p(1, 0, X)), (1, 2), 3)
+    scan_s(1, 0)
+    e = scan_s(1, 1)
+    gather(0, *ALL, e, ((0, LEFT),), 3)
+    quant_a(2, 4, "da2")
+    gather(1, *ALL, e, ((0, LEFT),), 2)
+    scan_p(1, 0)
+    e = scan_p(1, 1)
+    gather(0, *ALL, e, ((2, RIGHT),), 3)
+    e = middles(0, e)
+    ga0 = gather(0, *ALL, e, ((1, MID),), 3)
+    ga1 = gather(1, *ALL, e, ((1, MID),), 2)
     vw(ev[2])
-    gather(2, *CUTS[0], scans_s(2, 0, X), (0,), 2)
-    e2 = middles(2, scans_p(2, 0, X))
-    l0 = largest(0, 0, SL, 3, T.m3, ga0)
-    ga2 = [gather(2, *CUTS[0], e2, (1,), 2)]
+    for n in (0, 1):
+        scan_s(2, n)
+        scan_p(2, n)
     vw(ev[3])
-    gather(3, *CUTS[0], scans_s(3, 0, X), (0,), 2)
-    take3(0, l0)
-    l1 = []
-    e = middles(3, scans_p(3, 0, X, (None, lambda: l1.append(largest(1, 0, SL, 3, T.m3, ga1)))))
-    ga3 = [gather(3, *CUTS[0], e, (1,), 2)]
-    e_t = take3(1, l1[0])
-    for c in CUTS[1:]:
-        ga2.append(gather(2, *c, e2, (0, 1), 2))
-        ga3.append(gather(3, *c, e, (0, 1), 2))
+    for n in (0, 1):
+        e = scan_s(3, n)
+    gather(2, *EARLY, e, ((0, LEFT),), 2)
+    gather(3, *EARLY, e, ((0, LEFT),), 2)
+    for n in (0, 1):
+        e = scan_p(3, n)
+    g2 = [gather(2, *EARLY, e, ((1, RIGHT),), 2)]
+    g3 = [gather(3, *EARLY, e, ((1, RIGHT),), 2)]
+    middles(1, e)
+    take(0, *ALL, 3, largest(0, *ALL, 3, ga0))
+    for i, gl in ((2, g2), (3, g3)):
+        gl += 2 * [gather(i, *REST, e, ((0, LEFT), (1, RIGHT)), 2)]
+    join(1, *ALL, 2, RIGHT, largest(1, *ALL, 2, ga1))
 
     def pieces(n):
-        comb2(2, *CUTS[n], ga2[n])
-        vw(comb2(3, *CUTS[n], ga3[n]), e_t)
+        c = CUTS[n]
+        a = largest(2, *c, 2, g2[n])
+        b = largest(3, *c, 2, g3[n])
+        join(2, *c, 2, MID, a)
+        vw(join(3, *c, 2, MID, b))
 
     def dst(r):
         rid, pnc, _ = topo.addr(T.cores[r])
@@ -366,7 +396,7 @@ def rank_program(g, core, T, topo):
         ev_ = mm(bv, n, T.uvq[:, 128:256], T.uvc[:, 128:256], x, xc)
         eu = mm(bu, n, T.uvq[:, 0:128], T.uvc[:, 0:128], x, xc)
         need(act, "a", ev_)
-        a = done(act.activation(T.zvs[:, at:at + m], T.ps[:, 512 * bv + skip:512 * bv + skip + m], F.Copy), "sa")
+        a = S(act.activation(T.zvs[:, at:at + m], T.ps[:, 512 * bv + skip:512 * bv + skip + m], F.Copy))
         vw(eu)
         b = V(v.tensor_copy(T.zus[:, at:at + m], T.ps[:, 512 * bu + skip:512 * bu + skip + m]))
         return a, b
@@ -377,15 +407,17 @@ def rank_program(g, core, T, topo):
     prod(T.rq[:, 96:288], T.rc[:, 96:288], 192, 0, 192, 96, 7, 0)
     need(ten, "t", ("arrl", 16))
     a, b = prod(T.rq[:, 0:128], T.rc[:, 0:128], 128, 0, CAPP, 0, 1, 2)
+    H = 96
     need(act, "a", a, e_f)
-    H = P // 2
-    a = [done(act.activation(T.y1[:, c:c + H], T.zvs[:].indirect(T.offf[:, c // 16:(c + H) // 16]), F.Copy), "sa") for c in (0, H)]
-    vw(b, e_g, e3)
-    for n, c in enumerate((0, H)):
-        vw(a[n])
-        e = V(v.tensor_tensor(T.ys[:, c:c + H], T.zus[:].indirect(T.offg[:, c // 16:(c + H) // 16]), T.y1[:, c:c + H], A.add))
-        need(sy, "s", e)
-        sy.dma_start(T.y[:, c:c + H], T.ys[:, c:c + H]).then_inc(s.dy, 16)
+    e = S(act.activation(T.y1[:, H:P], T.zvs[:].indirect(T.offf[:, H // 16:P // 16]), F.Copy))
+    vw(a, b, e_g, e3)
+    vw(V(v.tensor_copy(T.y1[:, 0:H], T.zvs[:].indirect(T.offf[:, 0:H // 16]))))
+    for c, d in ((0, H), (H, P)):
+        if c:
+            vw(e)
+        o = V(v.tensor_tensor(T.ys[:, c:d], T.zus[:].indirect(T.offg[:, c // 16:d // 16]), T.y1[:, c:d], A.add))
+        need(sy, "s", o)
+        sy.dma_start(T.y[:, c:d], T.ys[:, c:d]).then_inc(s.dy, 16)
     sy.wait_ge(s.dy, 32)
     g.wait_ge(s.loc, 32)
     for name in ("sv", "st", "sa", "sg"):

from concourse.bass import DstId, RemoteDMATransfer, IndirectOffsetOnAxis
from concourse.mybir import dt, AluOpType, ActivationFunctionType

A = AluOpType
F = ActivationFunctionType
N = 4
CAPP = 96
P = 256
SL = N * CAPP
X = 512
LV = (2, 4)
P16, P4, H0, S4, S16, NT = 0, 1, 2, 3, 4, 5
PT = (P4, P16)
ST = (S4, S16)
NB = X // 16
RW = 2 * NB
NR = 35
CROW = 32
LEFT, MID, RIGHT = 0, 1, 2
CUTS = ((0, 2 * CAPP), (2 * CAPP, 3 * CAPP), (3 * CAPP, SL))
ALL, EARLY, REST = (0, SL), CUTS[0], (2 * CAPP, SL)

SCRATCH = {
    "xs": ("sbuf", [128, 2048], "bfloat16"),
    "ab": ("sbuf", [128, 2048], "bfloat16"),
    "uv": ("sbuf", [128, 1024], "bfloat16"),
    "xq": ("sbuf", [128, 512], "float8_e4m3fn_x4"),
    "xc": ("sbuf", [128, 512], "uint8"),
    "aq": ("sbuf", [128, 512], "float8_e4m3fn_x4"),
    "ac": ("sbuf", [128, 512], "uint8"),
    "uvq": ("sbuf", [128, 256], "float8_e4m3fn_x4"),
    "uvc": ("sbuf", [128, 256], "uint8"),
    "ps": ("psum", [128, 4096], "float32"),
    "tw": ("sbuf", [128, 4 * NT * X], "bfloat16"),
    "bm": ("sbuf", [128, 4 * RW], "bfloat16"),
    "bt": ("sbuf", [128, 2 * NR * RW], "bfloat16"),
    "mk": ("sbuf", [128, 2 * X], "bfloat16"),
    "mz": ("sbuf", [128, 5 * NB], "bfloat16"),
    "mi": ("sbuf", [128, 2 * SL], "bfloat16"),
    "one": ("sbuf", [128, 3 * SL], "bfloat16"),
    "m3": ("sbuf", [128, 3 * SL], "bfloat16"),
    "lnb": ("sbuf", [128, 24], "int32"),
    "lob": ("sbuf", [128, 24], "int32"),
    "wt": ("sbuf", [128, 2, 2, 3, 24], "int32"),
    "vt": ("sbuf", [128, 2, 2, 24], "float32"),
    "dd": ("sbuf", [128, 2, 24], "float32"),
    "cc": ("sbuf", [128, 2, 24], "float32"),
    "eq": ("sbuf", [128, 24], "float32"),
    "qq": ("sbuf", [128, 2, 24], "float32"),
    "mb": ("sbuf", [128, 2, 24], "float32"),
    "mc": ("sbuf", [128, 24], "float32"),
    "mx": ("sbuf", [128, 24], "float32"),
    "offl": ("sbuf", [128, 24], "uint16"),
    "offr": ("sbuf", [128, 24], "uint16"),
    "offm": ("sbuf", [128, 24], "uint16"),
    "ga": ("sbuf", [128, 12 * SL], "bfloat16"),
    "gb": ("sbuf", [128, 12 * SL], "bfloat16"),
    "t": ("sbuf", [128, 4 * SL], "bfloat16"),
    "tq": ("sbuf", [128, 192], "float8_e4m3fn_x4"),
    "tc": ("sbuf", [128, 192], "uint8"),
    "tq1": ("sbuf", [128, 128], "float8_e4m3fn_x4"),
    "tc1": ("sbuf", [128, 128], "uint8"),
    "tq2": ("sbuf", [128, 128], "float8_e4m3fn_x4"),
    "tc2": ("sbuf", [128, 128], "uint8"),
    "rq": ("sbuf", [128, 288], "float8_e4m3fn_x4"),
    "rc": ("sbuf", [128, 288], "uint8"),
    "pidx": ("sbuf", [128, 1], "int32"),
    "pid16": ("sbuf", [128, 1], "int32"),
    "pp": ("sbuf", [128, 32], "int32"),
    "pw": ("sbuf", [128, 32], "float32"),
    "pn": ("sbuf", [128, 16], "float32"),
    "offf": ("sbuf", [128, 16], "uint16"),
    "offg": ("sbuf", [128, 16], "uint16"),
    "zvs": ("sbuf", [128, SL], "float32"),
    "zus": ("sbuf", [128, SL + 8], "float32"),
    "y1": ("sbuf", [128, P], "float32"),
    "ys": ("sbuf", [128, P], "float32"),
}
SEMAPHORES = ["sv", "st", "sa", "sg", "dlo", "dln", "dx0", "dx1", "da0", "da1", "da2", "du", "dv", "dy",
              "gi", "arre", "arrl", "loc"]


def rank_program(g, core, T, topo):
    q = T.rank_of(core)
    if q is None:
        return
    v, ten, act, sy, s = g.vector, g.tensor, g.scalar, g.sync, T.sem
    cnt = {"sv": 0, "st": 0, "sa": 0, "sg": 0}
    seen = {}

    def done(ins, name):
        cnt[name] += 1
        ins.then_inc(s[name], 1)
        return (name, cnt[name])

    def need(eng, en, *evs):
        for name, val in evs:
            if seen.get((en, name), 0) < val:
                eng.wait_ge(s[name], val)
                seen[(en, name)] = val

    def V(ins):
        return done(ins, "sv")

    def S(ins):
        return done(ins, "sa")

    def vw(*evs):
        need(v, "v", *evs)

    sy.dma_start(T.lob[:], T.lo[:]).then_inc(s.dlo, 16)
    act.dma_start(T.lnb[:], T.ln[:]).then_inc(s.dln, 16)
    sy.dma_start(T.xs[:, 0:1024], T.x[:, 0:1024]).then_inc(s.dx0, 16)
    act.dma_start(T.ab[:, 0:512], T.a[:, 0:512]).then_inc(s.da0, 16)
    sy.dma_start(T.xs[:, 1024:2048], T.x[:, 1024:2048]).then_inc(s.dx1, 16)
    act.dma_start(T.ab[:, 512:1024], T.a[:, 512:1024]).then_inc(s.da1, 16)
    sy.dma_start(T.ab[:, 1024:2048], T.a[:, 1024:2048]).then_inc(s.da2, 16)
    act.dma_start(T.uv[:, 0:512], T.u[:]).then_inc(s.du, 16)
    sy.dma_start(T.uv[:, 512:1024], T.v[:]).then_inc(s.dv, 16)

    e_iota = done(g.iota(T.pidx[:], [[0, 1]], 0, 1), "sg")
    done(g.iota(T.mi[:], [[0, SL], [1, 2]], 0, 0, allow_small_or_imprecise_dtypes=True), "sg")
    e = done(g.iota(T.one[:], [[0, 3 * SL]], 1, 0, allow_small_or_imprecise_dtypes=True), "sg")
    need(g, "g", e)
    e_mi = done(g.affine_select(T.m3[:], T.one[:], [[0, SL], [1, 3]], A.not_equal, 0.0, 0, 0), "sg")

    V(v.memset(T.mk[:], 1.0))
    e = V(v.memset(T.mz[:], 1.0))
    for p in (0, 1):
        V(v.memset(T.bt[:, NR * RW * p:NR * RW * p + RW], 0.0))
    e3 = V(v.memset(T.zus[:, SL:SL + 8], 0.0))
    vw(e)
    for n, k in enumerate(LV):
        V(v.memset(T.mk[:, X * n:X * n + X:1 << k], 0.0))
    V(v.memset(T.mz[:, NB:2 * NB + 1:NB], 0.0))
    e_mk = V(v.memset(T.mz[:, 3 * NB + 1:4 * NB + 2:NB], 0.0))
    vw(e_iota)
    e_pid = V(v.tensor_scalar(T.pid16[:], T.pidx[:], 15, None, A.bitwise_and))
    need(g, "g", e_pid)
    for n, tab in enumerate((T.pf, T.pg)):
        g.indirect_dma_start(T.pp[:, 16 * n:16 * n + 16], None, tab[:], IndirectOffsetOnAxis(ap=T.pid16[:, 0:1], axis=0),
                             bounds_check=15).then_inc(s.gi, 16)

    vw(("dlo", 16), ("dln", 16))
    m = 6 * ((q + 1) % N)
    runs = [(0, m, 24)] + ([(24 - m, 0, m)] if m else [])
    for d, a, b in runs:
        V(v.tensor_copy(T.wt[:, 1, 0, 0, d:d + b - a], T.lob[:, a:b]))
        e = V(v.tensor_tensor(T.wt[:, 0, 0, 0, d:d + b - a], T.lnb[:, a:b], T.lob[:, a:b], A.add))
    vw(e)
    V(v.tensor_scalar(T.wt[:, 1, 1, 0], T.wt[:, 1, 0, 0], -1, None, A.add))
    e = V(v.tensor_scalar(T.wt[:, 0, 1, 0], T.wt[:, 0, 0, 0], -1, None, A.add))
    V(v.tensor_scalar(T.cc[:, 0], T.wt[:, 1, 0, 0], 0.5 / X, None, A.mult))
    vw(e)
    for n, k in enumerate(LV):
        e = V(v.tensor_scalar(T.wt[:, :, :, n + 1], T.wt[:, :, :, 0], k, None, A.arith_shift_right))
    V(v.tensor_scalar(T.cc[:, 1], T.wt[:, 0, 1, 0], -0.5 / X, -float(H0), A.mult, A.add))
    vw(e)
    V(v.tensor_tensor(T.vt[:], T.wt[:, 0, :, 1:3], T.wt[:, 1, :, 1:3], A.is_gt))
    e_dd = V(v.tensor_tensor(T.dd[:], T.wt[:, 0, 1, 1:3], T.wt[:, 1, 0, 1:3], A.subtract))
    vw(e_dd)

    def ends():
        for n in (0, 1):
            e = V(v.tensor_tensor(T.cc[:], T.cc[:], T.vt[:, :, n], A.add))
            vw(e)
        V(v.tensor_scalar(T.offl[:], T.cc[:, 0], 2.0 * X, None, A.mult))
        V(v.tensor_scalar(T.offr[:], T.cc[:, 1], -2.0 * X, None, A.mult))

    def middle_a():
        V(v.tensor_scalar(T.qq[:], T.dd[:], 2.0, None, A.is_ge))
        V(v.tensor_scalar(T.eq[:], T.dd[:, 1], 0.0, None, A.is_equal))
        V(v.tensor_scalar(T.mx[:], T.dd[:, 0], 3.0, float(RW), A.is_ge, A.mult))
        V(v.tensor_scalar(T.mb[:, 0], T.wt[:, 0, 1, 1], float(RW), float(RW * (CROW - 2)), A.mult, A.add))
        V(v.tensor_scalar(T.mb[:, 1], T.wt[:, 1, 0, 2], float(RW), float(RW - 1), A.mult, A.add))
        return V(v.tensor_scalar(T.mc[:], T.wt[:, 0, 1, 2], float(1 - 4 * RW), None, A.mult))

    def middle_b(e):
        vw(e)
        V(v.tensor_tensor(T.qq[:, 0], T.qq[:, 0], T.eq[:], A.mult))
        V(v.tensor_tensor(T.mb[:, 1], T.mb[:, 1], T.wt[:, 0, 1, 2], A.add))
        e = V(v.tensor_tensor(T.mx[:], T.mx[:], T.mc[:], A.add))
        vw(e)
        e = V(v.tensor_tensor(T.mb[:, 0], T.mb[:, 0], T.mx[:], A.add))
        vw(e)
        e = V(v.tensor_tensor(T.mb[:], T.mb[:], T.qq[:], A.mult))
        vw(e)
        e = V(v.tensor_tensor(T.mx[:], T.mb[:, 0], T.mb[:, 1], A.add))
        vw(e)
        return V(v.tensor_copy(T.offm[:], T.mx[:]))

    def quant(dst, sc, src):
        return V(v.quantize_mx(dst, sc, src))

    def mm(bank, n, w, wc, x, xc):
        return done(ten.matmul_mx(T.ps[:, 512 * bank:512 * bank + n], w, wc, x, xc, True, True), "st")

    def place(i, t):
        return X * (2 * (NT * (i // 2) + t) + i % 2)

    def col(i, t, a=0, b=X, st=1):
        o = place(i, t)
        return T.tw[:, o + a:o + b:st]

    def back(i, t, a, b):
        o = place(i, t)
        return T.tw[:, o + b - 1:(o + a - 1 if o + a else None):-1]

    def relu(i, a, b, bank):
        return S(act.activation(col(i, H0, a, b), T.ps[:, 512 * bank:512 * bank + b - a], F.Relu, scale=0.05))

    def prod_z(i, c0, c1, bank):
        return mm(bank, c1 - c0, T.aq[:, 128 * i:128 * i + 128], T.ac[:, 128 * i:128 * i + 128], T.xq[:, c0:c1], T.xc[:, c0:c1])

    vw(("da0", 16))
    quant(T.aq[:, 0:128], T.ac[:, 0:128], T.ab[:, 0:512])
    vw(("dx0", 16))
    e = quant(T.xq[:, 0:256], T.xc[:, 0:256], T.xs[:, 0:1024])
    need(ten, "t", e)
    z = prod_z(0, 0, 256, 0)
    need(act, "a", z)
    eh0 = relu(0, 0, 256, 0)
    ends()
    em = middle_a()
    ev = {}

    def quant_a(i0, i1, sem):
        vw((sem, 16))
        e = quant(T.aq[:, 128 * i0:128 * i1], T.ac[:, 128 * i0:128 * i1], T.ab[:, 512 * i0:512 * i1])
        need(ten, "t", e)
        for i in range(i0, i1):
            z = prod_z(i, 0, 512, i + 1)
            need(act, "a", z)
            ev[i] = relu(i, 0, 512, i + 1)

    def scan_s(i, n, a=0, b=X):
        return V(v.tensor_tensor_scan(back(i, ST[n], a, b), T.mk[:, X * n:X * n + b - a], back(i, H0, a, b), 0.0, A.mult, A.max))

    def scan_p(i, n, a=0, b=X):
        return V(v.tensor_tensor_scan(col(i, PT[n], a, b), T.mk[:, X * n:X * n + b - a], col(i, H0, a, b), 0.0, A.mult, A.max))

    def middles(p, e):
        i, o, b = 2 * p, NR * RW * p, 2 * RW * p
        vw(e)
        for c in (0, RW):
            e = V(v.tensor_copy(T.bm[:, b + c:b + c + RW], col(i, P16, 15, 2 * X, 16)))
        u, w = col(i, P4, 7, 2 * X, 16), col(i, P4, 11, 2 * X, 16)
        at = o + RW * CROW
        V(v.tensor_copy(T.bt[:, at:at + RW], u))
        V(v.tensor_copy(T.bt[:, at + RW:at + 2 * RW], w))
        V(v.tensor_tensor(T.bt[:, at + 2 * RW:at + 3 * RW], u, w, A.max))
        vw(e)
        for r in range(1, NB - 1, 2):
            e = V(v.tensor_tensor_scan(T.bt[:, o + RW * r:o + RW * (r + 2)], T.mz[:, NB - r:5 * NB - r], T.bm[:, b:b + 2 * RW],
                                       0.0, A.mult, A.max))
        return e

    def win(i, n):
        if n == MID:
            o = NR * RW * (i // 2)
            return T.bt[:, o + NB * (i % 2):o + NR * RW]
        a, b = (H0, S16) if n == LEFT else (P16, H0)
        return T.tw[:, place(i, a):place(i, b) + X]

    def off(n, c0, c1):
        return (T.offl, T.offm, T.offr)[n][:, c0 // 16:c1 // 16]

    def gather(i, c0, c1, after, ns, w):
        o = 3 * SL * i
        for at, n in ns:
            need(act, "a", after, e_off)
            e = S(act.activation(T.ga[:, o + w * c0 + at:o + w * c1:w], win(i, n).indirect(off(n, c0, c1)), F.Copy))
        return e

    def largest(i, c0, c1, w, e):
        vw(e, e_mi)
        o = 3 * SL * i
        return V(v.tensor_tensor_scan(T.gb[:, o + w * c0:o + w * c1], (T.mi if w == 2 else T.m3)[:, w * c0:w * c1],
                                      T.ga[:, o + w * c0:o + w * c1], 0.0, A.mult, A.max))

    def last(i, c0, c1, w):
        o = 3 * SL * i
        return T.gb[:, o + w * c0 + w - 1:o + w * c1:w]

    def piece(i, c0, c1):
        return T.t[:, 4 * c0 + i:4 * c1:4]

    def take(i, c0, c1, w, e):
        vw(e)
        return V(v.tensor_copy(piece(i, c0, c1), last(i, c0, c1, w)))

    def join(i, c0, c1, w, n, e):
        vw(e, e_off)
        return V(v.tensor_tensor(piece(i, c0, c1), win(i, n).indirect(off(n, c0, c1)), last(i, c0, c1, w), A.max))

    vw(e_mk, eh0)
    for n in (0, 1):
        scan_p(0, n, 0, 256)
        scan_s(0, n, 0, 256)
    vw(("dx1", 16))
    e = quant(T.xq[:, 256:512], T.xc[:, 256:512], T.xs[:, 1024:2048])
    need(ten, "t", e)
    z = prod_z(0, 256, 512, 1)
    need(act, "a", z)
    ev[0] = relu(0, 256, 512, 1)
    quant_a(1, 2, "da1")
    e_off = middle_b(em)
    vw(ev[0])
    for n in (0, 1):
        scan_s(0, n, 256, X)
        scan_p(0, n, 256, X)
    vw(ev[1])
    scan_s(1, 0)
    e = scan_s(1, 1)
    gather(0, *ALL, e, ((0, LEFT),), 3)
    quant_a(2, 4, "da2")
    gather(1, *ALL, e, ((0, LEFT),), 2)
    scan_p(1, 0)
    e = scan_p(1, 1)
    gather(0, *ALL, e, ((2, RIGHT),), 3)
    e = middles(0, e)
    ga0 = gather(0, *ALL, e, ((1, MID),), 3)
    ga1 = gather(1, *ALL, e, ((1, MID),), 2)
    vw(ev[2])
    for n in (0, 1):
        scan_s(2, n)
        scan_p(2, n)
    vw(ev[3])
    for n in (0, 1):
        e = scan_s(3, n)
    gather(2, *EARLY, e, ((0, LEFT),), 2)
    gather(3, *EARLY, e, ((0, LEFT),), 2)
    for n in (0, 1):
        e = scan_p(3, n)
    g2 = [gather(2, *EARLY, e, ((1, RIGHT),), 2)]
    g3 = [gather(3, *EARLY, e, ((1, RIGHT),), 2)]
    middles(1, e)
    take(0, *ALL, 3, largest(0, *ALL, 3, ga0))
    for i, gl in ((2, g2), (3, g3)):
        gl += 2 * [gather(i, *REST, e, ((0, LEFT), (1, RIGHT)), 2)]
    join(1, *ALL, 2, RIGHT, largest(1, *ALL, 2, ga1))

    def pieces(n):
        c = CUTS[n]
        a = largest(2, *c, 2, g2[n])
        b = largest(3, *c, 2, g3[n])
        join(2, *c, 2, MID, a)
        vw(join(3, *c, 2, MID, b))

    def dst(r):
        rid, pnc, _ = topo.addr(T.cores[r])
        return DstId(rid=rid, pnc=pnc)

    def send(js, sq, sc, c0, sem):
        for kind in (0, 1):
            tr = []
            for n, j in enumerate(js):
                r = (q + 1 + j) % N
                eng = topo.engines(core, T.cores[r])
                w = len(eng) // len(js)
                m = sum(1 << x for x in eng[n * w:n * w + w])
                a, b, at = c0 + n * CAPP, c0 + (n + 1) * CAPP, CAPP * (2 - j)
                if kind == 0:
                    sa, da = sq[:, a:b].bitcast(dt.uint8), T.rq[:, at:at + CAPP].bitcast(dt.uint8)
                else:
                    sa, da = sc[:, a:b], T.rc[:, at:at + CAPP]
                tr.append(RemoteDMATransfer(dst_ids=[dst(r)], dma_engine_mask=m, remote_sem=sem, src=sa, dst=da))
            g.remote_dma_fused(tr, local_sem=s.loc)

    pieces(0)
    e = quant(T.tq[:], T.tc[:], T.t[:, 0:768])
    need(g, "g", e)
    send([0, 1], T.tq, T.tc, 0, s.arre)
    pieces(1)
    e = quant(T.tq1[:], T.tc1[:], T.t[:, 640:1152])
    need(g, "g", e)
    send([2], T.tq1, T.tc1, 32, s.arrl)
    pieces(2)
    e_own = quant(T.tq2[:], T.tc2[:], T.t[:, 1024:1536])
    vw(("du", 16), ("dv", 16))
    e_uv = quant(T.uvq[:], T.uvc[:], T.uv[:])

    c1 = CAPP * (q + 1)
    vw(("gi", 32))
    V(v.tensor_scalar(T.pn[:], T.pp[:, 16:32], 0, 1 + c1, A.is_lt, A.mult))
    e = V(v.tensor_scalar(T.pw[:], T.pp[:], c1, SL, A.is_lt, A.mult))
    vw(e)
    e = V(v.tensor_tensor(T.pw[:], T.pw[:], T.pp[:], A.add))
    vw(e)
    e_f = V(v.tensor_scalar(T.offf[:], T.pw[:, 0:16], -c1, None, A.add))
    e = V(v.tensor_tensor(T.pn[:], T.pn[:], T.pw[:, 16:32], A.add))
    vw(e)
    e_g = V(v.tensor_scalar(T.offg[:], T.pn[:], -c1, None, A.add))

    def prod(x, xc, n, skip, m, at, bv, bu):
        ev_ = mm(bv, n, T.uvq[:, 128:256], T.uvc[:, 128:256], x, xc)
        eu = mm(bu, n, T.uvq[:, 0:128], T.uvc[:, 0:128], x, xc)
        need(act, "a", ev_)
        a = S(act.activation(T.zvs[:, at:at + m], T.ps[:, 512 * bv + skip:512 * bv + skip + m], F.Copy))
        vw(eu)
        b = V(v.tensor_copy(T.zus[:, at:at + m], T.ps[:, 512 * bu + skip:512 * bu + skip + m]))
        return a, b

    need(ten, "t", e_own, e_uv)
    prod(T.tq2[:], T.tc2[:], 128, 32, CAPP, 288, 5, 6)
    need(ten, "t", ("arre", 16), ev[3])
    prod(T.rq[:, 96:288], T.rc[:, 96:288], 192, 0, 192, 96, 7, 0)
    need(ten, "t", ("arrl", 16))
    a, b = prod(T.rq[:, 0:128], T.rc[:, 0:128], 128, 0, CAPP, 0, 1, 2)
    H = 96
    need(act, "a", a, e_f)
    e = S(act.activation(T.y1[:, H:P], T.zvs[:].indirect(T.offf[:, H // 16:P // 16]), F.Copy))
    vw(a, b, e_g, e3)
    vw(V(v.tensor_copy(T.y1[:, 0:H], T.zvs[:].indirect(T.offf[:, 0:H // 16]))))
    for c, d in ((0, H), (H, P)):
        if c:
            vw(e)
        o = V(v.tensor_tensor(T.ys[:, c:d], T.zus[:].indirect(T.offg[:, c // 16:d // 16]), T.y1[:, c:d], A.add))
        need(sy, "s", o)
        sy.dma_start(T.y[:, c:d], T.ys[:, c:d]).then_inc(s.dy, 16)
    sy.wait_ge(s.dy, 32)
    g.wait_ge(s.loc, 32)
    for name in ("sv", "st", "sa", "sg"):
        need(g, "g", (name, cnt[name]))
